import numpy as np, ml_dtypes
CORES = [33,38,57,62,81,86,161,166,185,190,209,214]
N = 12
import mx_ref
NC = 192
A = np.float32(0.03)
BF = ml_dtypes.bfloat16
def setup_inputs(rng):
    def f(*shape):
        return mx_ref.flush((rng.standard_normal(shape, dtype=np.float32) * np.exp2(rng.integers(-2, 3, shape[:-1] + (1,)))).astype(BF))
    tg = np.stack([rng.integers(0, N, (N, 128)), rng.integers(0, NC, (N, 128))], axis=2).astype(BF)
    return {"tg": tg, "x": f(N, 128, 512), "w": f(N, 128, 4 * NC)}
def setup_inputs_blocks(rng):
    d = setup_inputs(rng)
    for k in ("x", "w"): d[k] = mx_ref.spread(d[k], rng, 2)
    return d
def setup_inputs_sharp(rng):
    d = setup_inputs(rng); d["w"] = (d["w"].astype(np.float32) * 32).astype(BF)
    return d
def setup_inputs_apart(rng):
    d = setup_inputs(rng); d["w"] = mx_ref.flush((d["w"].astype(np.float32) * np.exp2(rng.permutation(np.linspace(-3, 3, N))).astype(np.float32).reshape(N, 1, 1)).astype(BF))
    return d
def reference(tg, x, w):
    W = [mx_ref.quantize(w[r]) for r in range(N)]
    y = np.zeros((N, 128, 2), np.float32)
    for j in range(N):
        X = mx_ref.quantize(x[j])
        L = [(mx_ref.matmul(X, W[r]) * A).astype(np.float64) for r in range(N)]
        m = np.max([l.max(axis=1, keepdims=True) for l in L], axis=0); s = sum(np.exp(l - m).sum(axis=1, keepdims=True) for l in L)
        t = np.array([[L[int(a) % N][i, int(c) % NC]] for i, (a, c) in enumerate(tg[j].astype(np.float32))])
        y[j] = np.concatenate([np.log(s) + m - t, np.log(s) + m], axis=1).astype(np.float32)
    return {"y": y}

@@ -1,0 +1,300 @@
+from concourse.bass import DstId, RemoteDMATransfer
+from concourse.mybir import dt, AluOpType as Op, AxisListType, ActivationFunctionType as Fn
+
+NC = 192
+NT = 128
+NW = 3 * NC
+A = 0.03
+D = 32.0
+MAGIC = 1.5 * D * 2.0 ** 23
+
+SCRATCH = {
+    "wt": ("sbuf", [128, 4 * NC], "bfloat16"),
+    "xt": ("sbuf", [128, 4 * NT], "bfloat16"),
+    "wc": ("sbuf", [128, NW], "float8_e4m3fn_x4"),
+    "wp": ("sbuf", [128, NW], "uint8"),
+    "xc": ("sbuf", [128, 4 * NT], "float8_e4m3fn_x4"),
+    "xp": ("sbuf", [128, 4 * NT], "uint8"),
+    "tgd": ("dram", [128, 2], "bfloat16"),
+    "tgin": ("dram", [3, 128, 2], "bfloat16"),
+    "tgs": ("sbuf", [128, 8], "bfloat16"),
+    "cn": ("sbuf", [128, NC], "bfloat16"),
+    "fl": ("sbuf", [128, 12], "bfloat16"),
+    "mk": ("sbuf", [128, 4 * NW], "bfloat16"),
+    "pr": ("sbuf", [128, 4 * NW], "float32"),
+    "ex": ("sbuf", [128, 4 * NW], "float32"),
+    "ps": ("psum", [128, 512 * 8], "float32"),
+    "mx": ("sbuf", [128, 8], "float32"),
+    "rr": ("sbuf", [128, 8], "float32"),
+    "e0": ("sbuf", [128, 1], "float32"),
+    "e1": ("sbuf", [128, 1], "float32"),
+    "e2": ("sbuf", [128, 1], "float32"),
+    "st": ("sbuf", [128, 24], "float32"),
+    "land": ("sbuf", [128, 32], "float32"),
+    "fb": ("sbuf", [128, 1], "float32"),
+    "ft": ("sbuf", [128, 1], "float32"),
+    "fd": ("sbuf", [128, 8], "float32"),
+    "fk": ("sbuf", [128, 8], "float32"),
+    "fq": ("sbuf", [128, 8], "float32"),
+    "fp": ("sbuf", [128, 16], "float32"),
+    "fs": ("sbuf", [128, 1], "float32"),
+    "fz": ("sbuf", [128, 1], "float32"),
+    "yo": ("sbuf", [128, 2], "float32"),
+}
+SEMAPHORES = ["ld_w", "ld_x", "ld_t", "ld_o", "ld_f", "st_y", "cn_ok", "v", "s", "pe", "snd", "tgin_ok", "rly",
+              "w1", "w2", "x1", "x2", "x3", "st1", "st2", "st3"]
+
+
+def bits(mask):
+    return [i for i in range(32) if (mask >> i) & 1]
+
+
+def unbits(lst):
+    return sum(1 << i for i in lst)
+
+
+def same_chip(topo, a, b):
+    return (topo.host(a), topo.chip(a)) == (topo.host(b), topo.chip(b))
+
+
+def xslot(topo, at, src):
+    if at == src:
+        return 0
+    if same_chip(topo, at, src):
+        return 1
+    return 2 if topo.die(at) == topo.die(src) else 3
+
+
+def row(topo, cores, a):
+    return sorted([c for c in cores if topo.chip(c) == topo.chip(a)], key=lambda c: xslot(topo, a, c))
+
+
+def column(topo, cores, a):
+    o = [c for c in cores if c != a and topo.host(c) == topo.host(a) and topo.die(c) == topo.die(a)]
+    o.sort(key=lambda c: (not topo.same_plane(a, c), c))
+    return [a] + o
+
+
+def w_plan(topo, cores, a, everyone):
+    dests = column(topo, cores, a)[1:]
+    cross = [d for d in dests if not topo.same_plane(a, d)]
+    own = [d for d in dests if d not in cross]
+    hs = [h for h in everyone if topo.die(h) == topo.die(a) and h not in cores and all(topo.may_write(h, d) for d in cross)]
+    if all(topo.may_write(a, d) for d in cross):
+        return {"codes": ([d for d in dests if d != cross[0]], {hs[0]: [cross[0]]}), "scales": (dests, {})}
+    return {"codes": (own, {hs[0]: cross}), "scales": (own, {hs[1]: cross})}
+
+
+def masks(topo, a, far, near):
+    lo = topo.mask(a, far)
+    return lo, topo.mask(a, near) & ~lo
+
+
+def wview(T, what, at):
+    if what == "codes":
+        return T.wc[:, at * NC:(at + 1) * NC].bitcast(dt.uint8)
+    return T.wp[:, at * NC:(at + 1) * NC]
+
+
+def xview(T, what, at):
+    if what == "codes":
+        return T.xc[:, at * NT:(at + 1) * NT].bitcast(dt.uint8)
+    return T.xp[:, at * NT:(at + 1) * NT]
+
+
+def fused(g, core, T, topo, cnt, tl):
+    g.remote_dma_fused([RemoteDMATransfer(dst_ids=[DstId(rid=topo.addr(d, core)[0], pnc=topo.addr(d, core)[1]) for d, _ in ds],
+                                          dma_engine_mask=m, remote_sem=sem, srcs=[src], dsts=[w for _, w in ds])
+                        for m, src, sem, ds in tl], local_sem=T.sem.snd)
+    cnt["snd"] += sum(len(bits(t[0])) for t in tl)
+
+
+def w_transfers(T, topo, cores, a, what, dests, mask):
+    by = {}
+    for d in dests:
+        by.setdefault(column(topo, cores, d).index(a), []).append(d)
+    return [(mask, wview(T, what, 0), T.sem["w%d" % s], [(d, wview(T, what, s)) for d in by[s]]) for s in sorted(by)]
+
+
+def helper_program(g, core, T, topo, everyone):
+    cores = list(T.cores)
+    for a in everyone:
+        if a not in cores or topo.die(a) != topo.die(core):
+            continue
+        r = row(topo, cores, a)
+        lo, hi = masks(topo, a, r[2], r[1])
+        plan = w_plan(topo, cores, a, everyone)
+        for what in ("codes", "scales"):
+            direct, relayed = plan[what]
+            if core in relayed:
+                g.wait_ge(T.sem.rly, len(bits(hi if direct else lo | hi)))
+                cnt = {"snd": 0}
+                for t in w_transfers(T, topo, cores, a, what, relayed[core], topo.mask(core, relayed[core][0])):
+                    fused(g, core, T, topo, cnt, [t])
+                g.wait_ge(T.sem.snd, cnt["snd"])
+
+
+def rank_program(g, core, T, topo):
+    everyone = [c for c in range(256) if same_chip(topo, c, core)]
+    if T.rank_of(core) is None:
+        helper_program(g, core, T, topo, everyone)
+        return
+    cores = list(T.cores)
+    R = row(topo, cores, core)
+    C = column(topo, cores, core)
+    lo, hi = masks(topo, core, R[2], R[1])
+    nlo, nhi = len(bits(lo)), len(bits(hi))
+    plan = w_plan(topo, cores, core, everyone)
+    early = 2 if topo.same_plane(core, C[1]) else 1
+    spans = [(0, early * NC), (early * NC, NW)]
+    cnt = {"v": 0, "s": 0, "snd": 0}
+
+    def vi(ins):
+        ins.then_inc(T.sem.v, 1)
+        cnt["v"] += 1
+        return cnt["v"]
+
+    def si(ins):
+        ins.then_inc(T.sem.s, 1)
+        cnt["s"] += 1
+        return cnt["s"]
+
+    g.sync.dma_start(T.wt[:], T.w[:]).then_inc(T.sem.ld_w, 16)
+    g.sync.dma_start(T.tgs[:, 0:2], T.tg[:]).then_inc(T.sem.ld_o, 16)
+    g.scalar.dma_start(T.tgd[:], T.tg[:]).then_inc(T.sem.ld_t, 16)
+    g.scalar.dma_start(T.xt[:], T.x[:]).then_inc(T.sem.ld_x, 16)
+    g.sync.wait_ge(T.sem.tgin_ok, 2 * nlo + nhi)
+    for k in (1, 2, 3):
+        g.sync.dma_start(T.tgs[:, 2 * k:2 * k + 2], T.tgin[k - 1]).then_inc(T.sem.ld_f, 16)
+
+    v = g.vector
+    i_e0 = vi(v.memset(T.e0[:], -D))
+    vi(v.memset(T.st[:], 0.0))
+    vi(v.memset(T.land[:, 0:8], 0.0))
+    v.wait_ge(T.sem.ld_w, 16)
+    i_qw = vi(v.quantize_mx(T.wc[:, 0:NC], T.wp[:, 0:NC], T.wt[:]))
+    v.wait_ge(T.sem.ld_x, 16)
+    i_qx = vi(v.quantize_mx(T.xc[:, 0:NT], T.xp[:, 0:NT], T.xt[:]))
+
+    def build_masks(k0, k1):
+        for s in range(3):
+            i = vi(v.tensor_scalar(T.fl[:, 4 * s + k0:4 * s + k1], T.tgs[:, 2 * k0:2 * k1:2], float(T.rank_of(C[s])), None, Op.is_equal))
+        v.wait_ge(T.sem.v, i)
+        for k in range(k0, k1):
+            for s in range(3):
+                o = k * NW + s * NC
+                vi(v.tensor_scalar(T.mk[:, o:o + NC], T.cn[:], T.tgs[:, 2 * k + 1:2 * k + 2],
+                                   T.fl[:, 4 * s + k:4 * s + k + 1], Op.is_equal, Op.mult))
+    v.wait_ge(T.sem.cn_ok, 1)
+    v.wait_ge(T.sem.ld_o, 16)
+    build_masks(0, 1)
+    v.wait_ge(T.sem.ld_f, 48)
+    build_masks(1, 4)
+    v.wait_ge(T.sem.v, cnt["v"])
+
+    groups = [(0, 0), (1, 0), (2, 0), (3, 0), (2, 1), (3, 1), (1, 1), (0, 1)]
+    pe = g.tensor
+    seen = set()
+
+    def pe_wait(name, n):
+        if name not in seen:
+            seen.add(name)
+            pe.wait_ge(T.sem[name], n)
+    pe_wait("v", i_qx)
+    for i, (k, h) in enumerate(groups):
+        c0, c1 = spans[h]
+        for s in range(c0 // NC, c1 // NC):
+            if s:
+                pe_wait("w%d" % s, 2 * nlo)
+        if k:
+            pe_wait("x%d" % k, 2 * (nhi if k == 1 else nlo))
+        pe.matmul_mx(T.ps[:, 512 * i:512 * i + c1 - c0], T.xc[:, k * NT:(k + 1) * NT], T.xp[:, k * NT:(k + 1) * NT],
+                     T.wc[:, c0:c1], T.wp[:, c0:c1], True, True).then_inc(T.sem.pe, 1)
+
+    shift_at = []
+    for i, (k, h) in enumerate(groups):
+        c0, c1 = spans[h]
+        P = T.ps[:, 512 * i:512 * i + c1 - c0]
+        o = k * NW
+        v.wait_ge(T.sem.pe, i + 1)
+        j = vi(v.tensor_reduce(T.mx[:, i:i + 1], P, AxisListType.X, Op.max))
+        vi(v.tensor_tensor(T.pr[:, o + c0:o + c1], P, T.mk[:, o + c0:o + c1], Op.mult))
+        v.wait_ge(T.sem.v, j)
+        shift_at.append(vi(v.tensor_scalar(T.rr[:, i:i + 1], T.mx[:, i:i + 1], -A, MAGIC, Op.mult, Op.add)))
+
+    sc = g.scalar
+    sc.wait_ge(T.sem.v, i_e0)
+    i_e1 = si(sc.activation(T.e1[:], T.e0[:], Fn.Exp))
+    done_at = {}
+    for i, (k, h) in enumerate(groups):
+        c0, c1 = spans[h]
+        P = T.ps[:, 512 * i:512 * i + c1 - c0]
+        o = k * NW
+        q = 4 * h if k == 0 else 8 * (k - 1) + 4 * h
+        buf = T.land if k == 0 else T.st
+        sc.wait_ge(T.sem.v, shift_at[i])
+        j = si(sc.activation(buf[:, q:q + 1], T.rr[:, i:i + 1], Fn.Identity, bias=-MAGIC))
+        si(sc.activation(T.pr[:, o + c0:o + c1], T.pr[:, o + c0:o + c1], Fn.Copy, scale=A, accum_out=buf[:, q + 2:q + 3]))
+        sc.wait_ge(T.sem.s, j)
+        done_at[(k, h)] = si(sc.activation(T.ex[:, o + c0:o + c1], P, Fn.Exp, bias=buf[:, q:q + 1], scale=A,
+                                           accum_out=buf[:, q + 1:q + 2]))
+    si(sc.activation(T.e2[:], T.e1[:], Fn.Ln))
+
+    g.iota(T.cn[:], [[1, NC]], 0, 0, allow_small_or_imprecise_dtypes=True).then_inc(T.sem.cn_ok, 1)
+
+    def send(tl):
+        fused(g, core, T, topo, cnt, tl)
+    at = {k: xslot(topo, R[k], core) for k in (1, 2, 3)}
+    g.wait_ge(T.sem.ld_t, 16)
+    send([(lo, T.tgd[:], T.sem.tgin_ok, [(R[k], T.tgin[at[k] - 1]) for k in (2, 3)]),
+          (hi, T.tgd[:], T.sem.tgin_ok, [(R[1], T.tgin[at[1] - 1])])])
+    g.wait_ge(T.sem.v, i_qw)
+    for what in ("codes", "scales"):
+        direct, relayed = plan[what]
+        tl = [(hi if direct else lo | hi, wview(T, what, 0), T.sem.rly, [(h, wview(T, what, 0)) for h in relayed])] if relayed else []
+        for t in w_transfers(T, topo, cores, core, what, direct, lo):
+            send(tl + [t])
+            tl = []
+        if tl:
+            send(tl)
+    g.wait_ge(T.sem.v, i_qx)
+    for k in (2, 3):
+        for what in ("codes", "scales"):
+            tl = [(lo, xview(T, what, 0), T.sem["x%d" % at[k]], [(R[k], xview(T, what, at[k]))])]
+            if k == 2:
+                tl.append((hi, xview(T, what, 0), T.sem["x%d" % at[1]], [(R[1], xview(T, what, at[1]))]))
+            send(tl)
+    b = bits(lo)
+    part = {1: hi, 2: unbits(b[:nlo // 2]), 3: unbits(b[nlo // 2:])}
+    for ks in ((2, 3), (1,)):
+        g.wait_ge(T.sem.s, max(done_at[(k, 1)] for k in ks))
+        send([(part[k], T.st[:, 8 * (k - 1):8 * k], T.sem["st%d" % at[k]], [(R[k], T.land[:, 8 * at[k]:8 * at[k] + 8])]) for k in ks])
+    g.wait_ge(T.sem.snd, cnt["snd"])
+
+    v.wait_ge(T.sem.s, done_at[(0, 1)])
+    v.wait_ge(T.sem.st1, nhi)
+    v.wait_ge(T.sem.st2, nlo // 2)
+    v.wait_ge(T.sem.st3, nlo // 2)
+    B, S, TL = T.land[:, 0:32:4], T.land[:, 1:32:4], T.land[:, 2:32:4]
+    j = vi(v.tensor_reduce(T.fb[:], B, AxisListType.X, Op.min))
+    v.wait_ge(T.sem.v, j)
+    j = vi(v.tensor_scalar(T.fd[:], B, T.fb[:], None, Op.subtract))
+    v.wait_ge(T.sem.v, j)
+    jk = vi(v.tensor_scalar(T.fk[:], T.fd[:], D / 2, None, Op.is_lt))
+    jq = vi(v.tensor_scalar(T.fq[:], T.fd[:], D, T.e1[:], Op.is_equal, Op.mult))
+    v.wait_ge(T.sem.v, jk)
+    vi(v.tensor_tensor(T.fp[:, 0:8], T.fk[:], S, Op.mult))
+    v.wait_ge(T.sem.v, jq)
+    j = vi(v.tensor_tensor(T.fp[:, 8:16], T.fq[:], S, Op.mult))
+    v.wait_ge(T.sem.v, j)
+    j = vi(v.tensor_reduce(T.fs[:], T.fp[:], AxisListType.X, Op.add))
+    jt = vi(v.tensor_reduce(T.ft[:], TL, AxisListType.X, Op.add))
+    sc.wait_ge(T.sem.v, j)
+    j = si(sc.activation(T.fz[:], T.fs[:], Fn.Ln))
+    v.wait_ge(T.sem.v, jt)
+    v.wait_ge(T.sem.s, j)
+    vi(v.tensor_scalar(T.yo[:, 0:1], T.fz[:], T.fb[:], T.ft[:], Op.subtract, Op.subtract))
+    j = vi(v.tensor_scalar(T.yo[:, 1:2], T.fz[:], T.fb[:], None, Op.subtract))
+    g.sync.wait_ge(T.sem.v, j)
+    g.sync.dma_start(T.y[:], T.yo[:]).then_inc(T.sem.st_y, 16)
+    g.sync.wait_ge(T.sem.st_y, 16)

@@ -7,6 +7,7 @@ NW = 3 * NC
 A = 0.03
 D = 32.0
 MAGIC = 1.5 * D * 2.0 ** 23
+BIG = 2.0 ** 96
 
 SCRATCH = {
     "wt": ("sbuf", [128, 4 * NC], "bfloat16"),
@@ -15,34 +16,32 @@ SCRATCH = {
     "wp": ("sbuf", [128, NW], "uint8"),
     "xc": ("sbuf", [128, 4 * NT], "float8_e4m3fn_x4"),
     "xp": ("sbuf", [128, 4 * NT], "uint8"),
-    "tgd": ("dram", [128, 2], "bfloat16"),
-    "tgin": ("dram", [3, 128, 2], "bfloat16"),
     "tgs": ("sbuf", [128, 8], "bfloat16"),
     "cn": ("sbuf", [128, NC], "bfloat16"),
-    "fl": ("sbuf", [128, 12], "bfloat16"),
+    "key": ("sbuf", [128, 4], "float32"),
     "mk": ("sbuf", [128, 4 * NW], "bfloat16"),
     "pr": ("sbuf", [128, 4 * NW], "float32"),
     "ex": ("sbuf", [128, 4 * NW], "float32"),
     "ps": ("psum", [128, 512 * 8], "float32"),
-    "mx": ("sbuf", [128, 8], "float32"),
-    "rr": ("sbuf", [128, 8], "float32"),
+    "mx": ("sbuf", [128, 22], "float32"),
+    "mg": ("sbuf", [128, 2], "float32"),
     "e0": ("sbuf", [128, 1], "float32"),
     "e1": ("sbuf", [128, 1], "float32"),
     "e2": ("sbuf", [128, 1], "float32"),
-    "st": ("sbuf", [128, 24], "float32"),
-    "land": ("sbuf", [128, 32], "float32"),
-    "fb": ("sbuf", [128, 1], "float32"),
+    "st": ("sbuf", [128, 48], "float32"),
+    "land": ("sbuf", [128, 48], "float32"),
+    "fb": ("sbuf", [128, 2], "float32"),
     "ft": ("sbuf", [128, 1], "float32"),
-    "fd": ("sbuf", [128, 8], "float32"),
-    "fk": ("sbuf", [128, 8], "float32"),
-    "fq": ("sbuf", [128, 8], "float32"),
-    "fp": ("sbuf", [128, 16], "float32"),
+    "fk": ("sbuf", [128, 12], "float32"),
+    "fq": ("sbuf", [128, 12], "float32"),
+    "fe": ("sbuf", [128, 12], "float32"),
+    "fp": ("sbuf", [128, 24], "float32"),
     "fs": ("sbuf", [128, 1], "float32"),
     "fz": ("sbuf", [128, 1], "float32"),
     "yo": ("sbuf", [128, 2], "float32"),
 }
-SEMAPHORES = ["ld_w", "ld_x", "ld_t", "ld_o", "ld_f", "st_y", "cn_ok", "v", "s", "pe", "snd", "tgin_ok", "rly",
-              "w1", "w2", "x1", "x2", "x3", "st1", "st2", "st3"]
+SEMAPHORES = ["ld_w", "ld_x", "ld_t", "st_y", "cn_ok", "v", "s", "pe", "snd", "tgin", "rly", "xrl",
+              "w1", "w2", "x0", "x1", "x2", "x3", "st0", "st1", "st2", "st3"]
 
 
 def bits(mask):
@@ -57,37 +56,49 @@ def same_chip(topo, a, b):
     return (topo.host(a), topo.chip(a)) == (topo.host(b), topo.chip(b))
 
 
-def xslot(topo, at, src):
-    if at == src:
-        return 0
-    if same_chip(topo, at, src):
-        return 1
-    return 2 if topo.die(at) == topo.die(src) else 3
-
-
 def row(topo, cores, a):
-    return sorted([c for c in cores if topo.chip(c) == topo.chip(a)], key=lambda c: xslot(topo, a, c))
+    return sorted(c for c in cores if topo.chip(c) == topo.chip(a))
+
+
+def opposite(topo, cores, a):
+    return [c for c in row(topo, cores, a) if not same_chip(topo, a, c) and topo.die(c) != topo.die(a)][0]
+
+
+def owner(topo, cores, a):
+    return all(topo.may_write(a, c) for c in cores if c != a)
 
 
 def column(topo, cores, a):
-    o = [c for c in cores if c != a and topo.host(c) == topo.host(a) and topo.die(c) == topo.die(a)]
-    o.sort(key=lambda c: (not topo.same_plane(a, c), c))
-    return [a] + o
+    mine = [c for c in cores if topo.host(c) == topo.host(a)]
+    last = max(topo.chip(x) for x in mine if any(topo.same_plane(x, y) for y in mine))
+
+    def side(c):
+        return owner(topo, cores, c) != (topo.chip(c) == last)
+    return [c for c in mine if side(c) == side(a)]
 
 
-def w_plan(topo, cores, a, everyone):
-    dests = column(topo, cores, a)[1:]
-    cross = [d for d in dests if not topo.same_plane(a, d)]
-    own = [d for d in dests if d not in cross]
-    hs = [h for h in everyone if topo.die(h) == topo.die(a) and h not in cores and all(topo.may_write(h, d) for d in cross)]
-    if all(topo.may_write(a, d) for d in cross):
-        return {"codes": ([d for d in dests if d != cross[0]], {hs[0]: [cross[0]]}), "scales": (dests, {})}
-    return {"codes": (own, {hs[0]: cross}), "scales": (own, {hs[1]: cross})}
+def wslot(topo, cores, at, src):
+    if at == src:
+        return 0
+    o = [c for c in column(topo, cores, at) if c != at]
+    o.sort(key=lambda c: (not topo.same_plane(at, c), not owner(topo, cores, c), c))
+    return 1 + o.index(src)
 
 
-def masks(topo, a, far, near):
-    lo = topo.mask(a, far)
-    return lo, topo.mask(a, near) & ~lo
+def far_partners(topo, cores, a):
+    return [d for d in column(topo, cores, a) if d != a and not topo.may_write(a, d)]
+
+
+def helpers(topo, cores, a, everyone):
+    far = far_partners(topo, cores, a) + [opposite(topo, cores, a)]
+    return [h for h in everyone if topo.die(h) == topo.die(a) and h not in cores and all(topo.may_write(h, d) for d in far)][:2]
+
+
+def engines(topo, cores, a):
+    R = row(topo, cores, a)
+    lo = topo.mask(a, [c for c in R if not same_chip(topo, a, c)][0])
+    hi = topo.mask(a, [c for c in R if c != a and same_chip(topo, a, c)][0]) & ~lo
+    return lo, hi, hi if any(topo.may_write(a, d) for d in column(topo, cores, a) if d != a) else lo | hi
 
 
 def wview(T, what, at):
@@ -112,26 +123,28 @@ def fused(g, core, T, topo, cnt, tl):
 def w_transfers(T, topo, cores, a, what, dests, mask):
     by = {}
     for d in dests:
-        by.setdefault(column(topo, cores, d).index(a), []).append(d)
+        by.setdefault(wslot(topo, cores, d, a), []).append(d)
     return [(mask, wview(T, what, 0), T.sem["w%d" % s], [(d, wview(T, what, s)) for d in by[s]]) for s in sorted(by)]
 
 
 def helper_program(g, core, T, topo, everyone):
     cores = list(T.cores)
     for a in everyone:
-        if a not in cores or topo.die(a) != topo.die(core):
+        hs = helpers(topo, cores, a, everyone) if a in cores else []
+        if core not in hs:
             continue
-        r = row(topo, cores, a)
-        lo, hi = masks(topo, a, r[2], r[1])
-        plan = w_plan(topo, cores, a, everyone)
-        for what in ("codes", "scales"):
-            direct, relayed = plan[what]
-            if core in relayed:
-                g.wait_ge(T.sem.rly, len(bits(hi if direct else lo | hi)))
-                cnt = {"snd": 0}
-                for t in w_transfers(T, topo, cores, a, what, relayed[core], topo.mask(core, relayed[core][0])):
-                    fused(g, core, T, topo, cnt, [t])
-                g.wait_ge(T.sem.snd, cnt["snd"])
+        what = ("codes", "scales")[hs.index(core)]
+        lo, hi, hand = engines(topo, cores, a)
+        cnt = {"snd": 0}
+        me, d = row(topo, cores, a).index(a), opposite(topo, cores, a)
+        g.wait_ge(T.sem.xrl, len(bits(hi)) // 2)
+        fused(g, core, T, topo, cnt, [(topo.mask(core, d), xview(T, what, me), T.sem["x%d" % me], [(d, xview(T, what, me))])])
+        far = far_partners(topo, cores, a)
+        if far:
+            g.wait_ge(T.sem.rly, len(bits(hand)))
+            for t in w_transfers(T, topo, cores, a, what, far, topo.mask(core, far[0])):
+                fused(g, core, T, topo, cnt, [t])
+        g.wait_ge(T.sem.snd, cnt["snd"])
 
 
 def rank_program(g, core, T, topo):
@@ -141,12 +154,16 @@ def rank_program(g, core, T, topo):
         return
     cores = list(T.cores)
     R = row(topo, cores, core)
-    C = column(topo, cores, core)
-    lo, hi = masks(topo, core, R[2], R[1])
+    me = R.index(core)
+    near = [k for k in range(4) if k != me and same_chip(topo, core, R[k])]
+    away = [k for k in range(4) if not same_chip(topo, core, R[k])]
+    away.sort(key=lambda k: topo.die(R[k]) != topo.die(core))
+    C = sorted(column(topo, cores, core), key=lambda c: wslot(topo, cores, core, c))
+    lo, hi, hand = engines(topo, cores, core)
     nlo, nhi = len(bits(lo)), len(bits(hi))
-    plan = w_plan(topo, cores, core, everyone)
-    early = 2 if topo.same_plane(core, C[1]) else 1
-    spans = [(0, early * NC), (early * NC, NW)]
+    hi_a, hi_b = unbits(bits(hi)[::2]), unbits(bits(hi)[1::2])
+    hs = helpers(topo, cores, core, everyone)
+    straight = [d for d in C[1:] if topo.may_write(core, d)]
     cnt = {"v": 0, "s": 0, "snd": 0}
 
     def vi(ins):
@@ -159,142 +176,180 @@ def rank_program(g, core, T, topo):
         cnt["s"] += 1
         return cnt["s"]
 
-    g.sync.dma_start(T.wt[:], T.w[:]).then_inc(T.sem.ld_w, 16)
-    g.sync.dma_start(T.tgs[:, 0:2], T.tg[:]).then_inc(T.sem.ld_o, 16)
-    g.scalar.dma_start(T.tgd[:], T.tg[:]).then_inc(T.sem.ld_t, 16)
-    g.scalar.dma_start(T.xt[:], T.x[:]).then_inc(T.sem.ld_x, 16)
-    g.sync.wait_ge(T.sem.tgin_ok, 2 * nlo + nhi)
-    for k in (1, 2, 3):
-        g.sync.dma_start(T.tgs[:, 2 * k:2 * k + 2], T.tgin[k - 1]).then_inc(T.sem.ld_f, 16)
+    g.sync.dma_start(T.xt[:], T.x[:]).then_inc(T.sem.ld_x, 16)
+    g.scalar.dma_start(T.tgs[:, 2 * me:2 * me + 2], T.tg[:]).then_inc(T.sem.ld_t, 16)
+    g.scalar.dma_start(T.wt[:], T.w[:]).then_inc(T.sem.ld_w, 16)
 
-    v = g.vector
+    early, mid, late = [[(k, s, s + 1) for k in ks] for s, ks in enumerate((near + away, near + away, away + near))]
+    first, last = (me, 0, 1), (me, 1, 3)
+    foreign = early[:2] + mid[:2] + early[2:] + mid[2:] + late
+    groups = [first] + foreign + [last]
+    num = {gr: i for i, gr in enumerate(groups)}
+    bank = {gr: i if i < 7 else 7 if gr == last else num[(gr[0], 0, 1)] for i, gr in enumerate(groups)}
+    v, sc, pe = g.vector, g.scalar, g.tensor
+
+    def cols(gr):
+        k, s0, s1 = gr
+        return k * NW + s0 * NC, k * NW + s1 * NC
+
+    def psv(gr):
+        return T.ps[:, 512 * bank[gr]:512 * bank[gr] + (gr[2] - gr[1]) * NC]
+
+    def sums(gr):
+        return T.land if gr[0] == me else T.st, 12 * gr[0] + 4 * gr[1]
+
     i_e0 = vi(v.memset(T.e0[:], -D))
     vi(v.memset(T.st[:], 0.0))
-    vi(v.memset(T.land[:, 0:8], 0.0))
+    vi(v.memset(T.mx[:], 1.0))
+    vi(v.memset(T.mg[:, 0:1], MAGIC))
+    vi(v.memset(T.mg[:, 1:2], -MAGIC))
+    i_z = vi(v.memset(T.land[:, 12 * me:12 * me + 12], 0.0))
+    v.wait_ge(T.sem.v, i_z)
+    vi(v.memset(T.land[:, 12 * me + 9:12 * me + 10], BIG))
+    v.wait_ge(T.sem.ld_x, 16)
+    i_qx = vi(v.quantize_mx(T.xc[:, me * NT:(me + 1) * NT], T.xp[:, me * NT:(me + 1) * NT], T.xt[:]))
     v.wait_ge(T.sem.ld_w, 16)
     i_qw = vi(v.quantize_mx(T.wc[:, 0:NC], T.wp[:, 0:NC], T.wt[:]))
-    v.wait_ge(T.sem.ld_x, 16)
-    i_qx = vi(v.quantize_mx(T.xc[:, 0:NT], T.xp[:, 0:NT], T.xt[:]))
 
-    def build_masks(k0, k1):
-        for s in range(3):
-            i = vi(v.tensor_scalar(T.fl[:, 4 * s + k0:4 * s + k1], T.tgs[:, 2 * k0:2 * k1:2], float(T.rank_of(C[s])), None, Op.is_equal))
-        v.wait_ge(T.sem.v, i)
-        for k in range(k0, k1):
+    def v_masks(ks):
+        for k in ks:
+            j = vi(v.tensor_scalar(T.key[:, k:k + 1], T.tgs[:, 2 * k:2 * k + 1], float(NC), T.tgs[:, 2 * k + 1:2 * k + 2],
+                                   Op.mult, Op.add))
+        v.wait_ge(T.sem.v, j)
+        for k in ks:
             for s in range(3):
                 o = k * NW + s * NC
-                vi(v.tensor_scalar(T.mk[:, o:o + NC], T.cn[:], T.tgs[:, 2 * k + 1:2 * k + 2],
-                                   T.fl[:, 4 * s + k:4 * s + k + 1], Op.is_equal, Op.mult))
-    v.wait_ge(T.sem.cn_ok, 1)
-    v.wait_ge(T.sem.ld_o, 16)
-    build_masks(0, 1)
-    v.wait_ge(T.sem.ld_f, 48)
-    build_masks(1, 4)
-    v.wait_ge(T.sem.v, cnt["v"])
+                j = vi(v.tensor_scalar(T.mk[:, o:o + NC], T.cn[:], float(NC * T.rank_of(C[s])), T.key[:, k:k + 1],
+                                       Op.add, Op.is_equal))
+        return j
 
-    groups = [(0, 0), (1, 0), (2, 0), (3, 0), (2, 1), (3, 1), (1, 1), (0, 1)]
-    pe = g.tensor
+    def v_max(gr):
+        i = num[gr]
+        v.wait_ge(T.sem.pe, i + 1)
+        return vi(v.tensor_reduce(T.mx[:, 2 * i:2 * i + 1], psv(gr), AxisListType.X, Op.max))
+
+    def v_shift(gr, j):
+        i = num[gr]
+        buf, q = sums(gr)
+        v.wait_ge(T.sem.v, j)
+        return vi(v.tensor_tensor_scan(buf[:, q:q + 2], T.mx[:, 2 * i:2 * i + 2], T.mg[:], -A, Op.mult, Op.add))
+
+    def v_pick(gr):
+        a, b = cols(gr)
+        return vi(v.tensor_tensor(T.pr[:, a:b], psv(gr), T.mk[:, a:b], Op.mult))
+
+    def v_total(gr, j):
+        a, b = cols(gr)
+        buf, q = sums(gr)
+        v.wait_ge(T.sem.v, j)
+        return vi(v.tensor_reduce(buf[:, q + 3:q + 4], T.pr[:, a:b], AxisListType.X, Op.add))
+
+    def s_exp(gr, j):
+        a, b = cols(gr)
+        buf, q = sums(gr)
+        sc.wait_ge(T.sem.v, j)
+        return si(sc.activation(T.ex[:, a:b], psv(gr), Fn.Exp, bias=buf[:, q + 1:q + 2], scale=A, accum_out=buf[:, q + 2:q + 3]))
+
+    def s_total(gr, j):
+        a, b = cols(gr)
+        buf, q = sums(gr)
+        sc.wait_ge(T.sem.v, j)
+        return si(sc.activation(T.pr[:, a:b], T.pr[:, a:b], Fn.Copy, accum_out=buf[:, q + 3:q + 4]))
+
+    sc.wait_ge(T.sem.v, i_e0)
+    si(sc.activation(T.e1[:], T.e0[:], Fn.Exp))
+    v.wait_ge(T.sem.cn_ok, 1)
+    v.wait_ge(T.sem.ld_t, 16)
+    j = v_masks([me])
+    jm = v_max(first)
+    v.wait_ge(T.sem.v, j)
+    jp = v_pick(first)
+    s_exp(first, v_shift(first, jm))
+    v_total(first, jp)
+    v.wait_ge(T.sem.tgin, 2 * nlo + nhi)
+    j = v_masks(near + away)
+    v.wait_ge(T.sem.v, j)
+    freed, done_at = {}, {}
+    for gr in foreign:
+        k = gr[0]
+        jm = v_max(gr)
+        jp = v_pick(gr)
+        j = s_exp(gr, v_shift(gr, jm))
+        if gr in early:
+            freed[k] = jp, j
+        elif gr in mid:
+            s_total((k, 0, 2), jp)
+        else:
+            done_at[k] = s_total(gr, jp)
+    jm = v_max(last)
+    jp = v_pick(last)
+    i_own = s_exp(last, v_shift(last, jm))
+    v_total(last, jp)
+    si(sc.activation(T.e2[:], T.e1[:], Fn.Ln))
+
     seen = set()
 
     def pe_wait(name, n):
         if name not in seen:
             seen.add(name)
             pe.wait_ge(T.sem[name], n)
-    pe_wait("v", i_qx)
-    for i, (k, h) in enumerate(groups):
-        c0, c1 = spans[h]
-        for s in range(c0 // NC, c1 // NC):
-            if s:
-                pe_wait("w%d" % s, 2 * nlo)
-        if k:
-            pe_wait("x%d" % k, 2 * (nhi if k == 1 else nlo))
-        pe.matmul_mx(T.ps[:, 512 * i:512 * i + c1 - c0], T.xc[:, k * NT:(k + 1) * NT], T.xp[:, k * NT:(k + 1) * NT],
-                     T.wc[:, c0:c1], T.wp[:, c0:c1], True, True).then_inc(T.sem.pe, 1)
-
-    shift_at = []
-    for i, (k, h) in enumerate(groups):
-        c0, c1 = spans[h]
-        P = T.ps[:, 512 * i:512 * i + c1 - c0]
-        o = k * NW
-        v.wait_ge(T.sem.pe, i + 1)
-        j = vi(v.tensor_reduce(T.mx[:, i:i + 1], P, AxisListType.X, Op.max))
-        vi(v.tensor_tensor(T.pr[:, o + c0:o + c1], P, T.mk[:, o + c0:o + c1], Op.mult))
-        v.wait_ge(T.sem.v, j)
-        shift_at.append(vi(v.tensor_scalar(T.rr[:, i:i + 1], T.mx[:, i:i + 1], -A, MAGIC, Op.mult, Op.add)))
-
-    sc = g.scalar
-    sc.wait_ge(T.sem.v, i_e0)
-    i_e1 = si(sc.activation(T.e1[:], T.e0[:], Fn.Exp))
-    done_at = {}
-    for i, (k, h) in enumerate(groups):
-        c0, c1 = spans[h]
-        P = T.ps[:, 512 * i:512 * i + c1 - c0]
-        o = k * NW
-        q = 4 * h if k == 0 else 8 * (k - 1) + 4 * h
-        buf = T.land if k == 0 else T.st
-        sc.wait_ge(T.sem.v, shift_at[i])
-        j = si(sc.activation(buf[:, q:q + 1], T.rr[:, i:i + 1], Fn.Identity, bias=-MAGIC))
-        si(sc.activation(T.pr[:, o + c0:o + c1], T.pr[:, o + c0:o + c1], Fn.Copy, scale=A, accum_out=buf[:, q + 2:q + 3]))
-        sc.wait_ge(T.sem.s, j)
-        done_at[(k, h)] = si(sc.activation(T.ex[:, o + c0:o + c1], P, Fn.Exp, bias=buf[:, q:q + 1], scale=A,
-                                           accum_out=buf[:, q + 1:q + 2]))
-    si(sc.activation(T.e2[:], T.e1[:], Fn.Ln))
+    pe_wait("v", i_qw)
+    for gr in groups:
+        k, s0, s1 = gr
+        if k != me:
+            pe_wait("x%d" % k, nhi if k in near else 2 * nlo)
+        for s in range(max(s0, 1), s1):
+            pe_wait("w%d" % s, 2 * nlo)
+        if gr in late:
+            pe.wait_ge(T.sem.v, freed[k][0])
+            pe.wait_ge(T.sem.s, freed[k][1])
+        pe.matmul_mx(psv(gr), T.xc[:, k * NT:(k + 1) * NT], T.xp[:, k * NT:(k + 1) * NT],
+                     T.wc[:, s0 * NC:s1 * NC], T.wp[:, s0 * NC:s1 * NC], True, True).then_inc(T.sem.pe, 1)
 
     g.iota(T.cn[:], [[1, NC]], 0, 0, allow_small_or_imprecise_dtypes=True).then_inc(T.sem.cn_ok, 1)
 
     def send(tl):
         fused(g, core, T, topo, cnt, tl)
-    at = {k: xslot(topo, R[k], core) for k in (1, 2, 3)}
     g.wait_ge(T.sem.ld_t, 16)
-    send([(lo, T.tgd[:], T.sem.tgin_ok, [(R[k], T.tgin[at[k] - 1]) for k in (2, 3)]),
-          (hi, T.tgd[:], T.sem.tgin_ok, [(R[1], T.tgin[at[1] - 1])])])
-    g.wait_ge(T.sem.v, i_qw)
-    for what in ("codes", "scales"):
-        direct, relayed = plan[what]
-        tl = [(hi if direct else lo | hi, wview(T, what, 0), T.sem.rly, [(h, wview(T, what, 0)) for h in relayed])] if relayed else []
-        for t in w_transfers(T, topo, cores, core, what, direct, lo):
-            send(tl + [t])
-            tl = []
-        if tl:
-            send(tl)
+    view = T.tgs[:, 2 * me:2 * me + 2]
+    send([(lo, view, T.sem.tgin, [(R[k], view) for k in away]), (hi, view, T.sem.tgin, [(R[k], view) for k in near])])
     g.wait_ge(T.sem.v, i_qx)
-    for k in (2, 3):
-        for what in ("codes", "scales"):
-            tl = [(lo, xview(T, what, 0), T.sem["x%d" % at[k]], [(R[k], xview(T, what, at[k]))])]
-            if k == 2:
-                tl.append((hi, xview(T, what, 0), T.sem["x%d" % at[1]], [(R[1], xview(T, what, at[1]))]))
-            send(tl)
-    b = bits(lo)
-    part = {1: hi, 2: unbits(b[:nlo // 2]), 3: unbits(b[nlo // 2:])}
-    for ks in ((2, 3), (1,)):
-        g.wait_ge(T.sem.s, max(done_at[(k, 1)] for k in ks))
-        send([(part[k], T.st[:, 8 * (k - 1):8 * k], T.sem["st%d" % at[k]], [(R[k], T.land[:, 8 * at[k]:8 * at[k] + 8])]) for k in ks])
+    for h, what in zip(hs, ("codes", "scales")):
+        view, sem = xview(T, what, me), T.sem["x%d" % me]
+        send([(lo, view, sem, [(R[away[0]], view)]), (hi_a, view, sem, [(R[near[0]], view)]), (hi_b, view, T.sem.xrl, [(h, view)])])
+    g.wait_ge(T.sem.v, i_qw)
+    for h, what in zip(hs, ("codes", "scales")):
+        tl = [(hand, wview(T, what, 0), T.sem.rly, [(h, wview(T, what, 0))])] if far_partners(topo, cores, core) else []
+        send(tl + w_transfers(T, topo, cores, core, what, straight, lo))
+    for k in away + near:
+        g.wait_ge(T.sem.s, done_at[k])
+        send([(hi if k in near else lo, T.st[:, 12 * k:12 * k + 12], T.sem["st%d" % me], [(R[k], T.land[:, 12 * me:12 * me + 12])])])
     g.wait_ge(T.sem.snd, cnt["snd"])
 
-    v.wait_ge(T.sem.s, done_at[(0, 1)])
-    v.wait_ge(T.sem.st1, nhi)
-    v.wait_ge(T.sem.st2, nlo // 2)
-    v.wait_ge(T.sem.st3, nlo // 2)
-    B, S, TL = T.land[:, 0:32:4], T.land[:, 1:32:4], T.land[:, 2:32:4]
-    j = vi(v.tensor_reduce(T.fb[:], B, AxisListType.X, Op.min))
+    v.wait_ge(T.sem.s, i_own)
+    for k in near + away:
+        v.wait_ge(T.sem["st%d" % k], nhi if k in near else nlo)
+    v.wait_ge(T.sem.v, cnt["v"])
+    B, S, TL = T.land[:, 1:48:4], T.land[:, 2:48:4], T.land[:, 3:48:4]
+    j = vi(v.tensor_reduce(T.fb[:, 1:2], B, AxisListType.X, Op.min))
+    vi(v.tensor_scalar(T.fe[:], S, T.e1[:], None, Op.mult))
     v.wait_ge(T.sem.v, j)
-    j = vi(v.tensor_scalar(T.fd[:], B, T.fb[:], None, Op.subtract))
-    v.wait_ge(T.sem.v, j)
-    jk = vi(v.tensor_scalar(T.fk[:], T.fd[:], D / 2, None, Op.is_lt))
-    jq = vi(v.tensor_scalar(T.fq[:], T.fd[:], D, T.e1[:], Op.is_equal, Op.mult))
+    jk = vi(v.tensor_scalar(T.fk[:], B, T.fb[:, 1:2], D / 2, Op.subtract, Op.is_lt))
+    jq = vi(v.tensor_scalar(T.fq[:], B, T.fb[:, 1:2], D, Op.subtract, Op.is_equal))
     v.wait_ge(T.sem.v, jk)
-    vi(v.tensor_tensor(T.fp[:, 0:8], T.fk[:], S, Op.mult))
+    vi(v.tensor_tensor(T.fp[:, 0:12], T.fk[:], S, Op.mult))
     v.wait_ge(T.sem.v, jq)
-    j = vi(v.tensor_tensor(T.fp[:, 8:16], T.fq[:], S, Op.mult))
+    j = vi(v.tensor_tensor(T.fp[:, 12:24], T.fq[:], T.fe[:], Op.mult))
     v.wait_ge(T.sem.v, j)
     j = vi(v.tensor_reduce(T.fs[:], T.fp[:], AxisListType.X, Op.add))
     jt = vi(v.tensor_reduce(T.ft[:], TL, AxisListType.X, Op.add))
     sc.wait_ge(T.sem.v, j)
     j = si(sc.activation(T.fz[:], T.fs[:], Fn.Ln))
     v.wait_ge(T.sem.v, jt)
+    jt = vi(v.tensor_scalar(T.fb[:, 0:1], T.ft[:], A, T.fb[:, 1:2], Op.mult, Op.add))
+    v.wait_ge(T.sem.v, jt)
     v.wait_ge(T.sem.s, j)
-    vi(v.tensor_scalar(T.yo[:, 0:1], T.fz[:], T.fb[:], T.ft[:], Op.subtract, Op.subtract))
-    j = vi(v.tensor_scalar(T.yo[:, 1:2], T.fz[:], T.fb[:], None, Op.subtract))
+    j = vi(v.tensor_scalar(T.yo[:], T.fb[:], T.fz[:], -1.0, Op.subtract, Op.mult))
     g.sync.wait_ge(T.sem.v, j)
     g.sync.dma_start(T.y[:], T.yo[:]).then_inc(T.sem.st_y, 16)
     g.sync.wait_ge(T.sem.st_y, 16)

from concourse.bass import DstId, RemoteDMATransfer
from concourse.mybir import dt, AluOpType as Op, AxisListType, ActivationFunctionType as Fn

NC = 192
NT = 128
NW = 3 * NC
A = 0.03
D = 32.0
MAGIC = 1.5 * D * 2.0 ** 23
BIG = 2.0 ** 96

SCRATCH = {
    "wt": ("sbuf", [128, 4 * NC], "bfloat16"),
    "xt": ("sbuf", [128, 4 * NT], "bfloat16"),
    "wc": ("sbuf", [128, NW], "float8_e4m3fn_x4"),
    "wp": ("sbuf", [128, NW], "uint8"),
    "xc": ("sbuf", [128, 4 * NT], "float8_e4m3fn_x4"),
    "xp": ("sbuf", [128, 4 * NT], "uint8"),
    "tgs": ("sbuf", [128, 8], "bfloat16"),
    "cn": ("sbuf", [128, NC], "bfloat16"),
    "key": ("sbuf", [128, 4], "float32"),
    "mk": ("sbuf", [128, 4 * NW], "bfloat16"),
    "pr": ("sbuf", [128, 4 * NW], "float32"),
    "ex": ("sbuf", [128, 4 * NW], "float32"),
    "ps": ("psum", [128, 512 * 8], "float32"),
    "mx": ("sbuf", [128, 22], "float32"),
    "mg": ("sbuf", [128, 2], "float32"),
    "e0": ("sbuf", [128, 1], "float32"),
    "e1": ("sbuf", [128, 1], "float32"),
    "e2": ("sbuf", [128, 1], "float32"),
    "st": ("sbuf", [128, 48], "float32"),
    "land": ("sbuf", [128, 48], "float32"),
    "fb": ("sbuf", [128, 2], "float32"),
    "ft": ("sbuf", [128, 1], "float32"),
    "fk": ("sbuf", [128, 12], "float32"),
    "fq": ("sbuf", [128, 12], "float32"),
    "fe": ("sbuf", [128, 12], "float32"),
    "fp": ("sbuf", [128, 24], "float32"),
    "fs": ("sbuf", [128, 1], "float32"),
    "fz": ("sbuf", [128, 1], "float32"),
    "yo": ("sbuf", [128, 2], "float32"),
}
SEMAPHORES = ["ld_w", "ld_x", "ld_t", "st_y", "cn_ok", "v", "s", "pe", "snd", "tgin", "rly", "xrl",
              "w1", "w2", "x0", "x1", "x2", "x3", "st0", "st1", "st2", "st3"]


def bits(mask):
    return [i for i in range(32) if (mask >> i) & 1]


def unbits(lst):
    return sum(1 << i for i in lst)


def same_chip(topo, a, b):
    return (topo.host(a), topo.chip(a)) == (topo.host(b), topo.chip(b))


def row(topo, cores, a):
    return sorted(c for c in cores if topo.chip(c) == topo.chip(a))


def opposite(topo, cores, a):
    return [c for c in row(topo, cores, a) if not same_chip(topo, a, c) and topo.die(c) != topo.die(a)][0]


def owner(topo, cores, a):
    return all(topo.may_write(a, c) for c in cores if c != a)


def column(topo, cores, a):
    mine = [c for c in cores if topo.host(c) == topo.host(a)]
    last = max(topo.chip(x) for x in mine if any(topo.same_plane(x, y) for y in mine))

    def side(c):
        return owner(topo, cores, c) != (topo.chip(c) == last)
    return [c for c in mine if side(c) == side(a)]


def wslot(topo, cores, at, src):
    if at == src:
        return 0
    o = [c for c in column(topo, cores, at) if c != at]
    o.sort(key=lambda c: (not topo.same_plane(at, c), not owner(topo, cores, c), c))
    return 1 + o.index(src)


def far_partners(topo, cores, a):
    return [d for d in column(topo, cores, a) if d != a and not topo.may_write(a, d)]


def helpers(topo, cores, a, everyone):
    far = far_partners(topo, cores, a) + [opposite(topo, cores, a)]
    return [h for h in everyone if topo.die(h) == topo.die(a) and h not in cores and all(topo.may_write(h, d) for d in far)][:2]


def engines(topo, cores, a):
    R = row(topo, cores, a)
    lo = topo.mask(a, [c for c in R if not same_chip(topo, a, c)][0])
    hi = topo.mask(a, [c for c in R if c != a and same_chip(topo, a, c)][0]) & ~lo
    return lo, hi, hi if any(topo.may_write(a, d) for d in column(topo, cores, a) if d != a) else lo | hi


def wview(T, what, at):
    if what == "codes":
        return T.wc[:, at * NC:(at + 1) * NC].bitcast(dt.uint8)
    return T.wp[:, at * NC:(at + 1) * NC]


def xview(T, what, at):
    if what == "codes":
        return T.xc[:, at * NT:(at + 1) * NT].bitcast(dt.uint8)
    return T.xp[:, at * NT:(at + 1) * NT]


def fused(g, core, T, topo, cnt, tl):
    g.remote_dma_fused([RemoteDMATransfer(dst_ids=[DstId(rid=topo.addr(d, core)[0], pnc=topo.addr(d, core)[1]) for d, _ in ds],
                                          dma_engine_mask=m, remote_sem=sem, srcs=[src], dsts=[w for _, w in ds])
                        for m, src, sem, ds in tl], local_sem=T.sem.snd)
    cnt["snd"] += sum(len(bits(t[0])) for t in tl)


def w_transfers(T, topo, cores, a, what, dests, mask):
    by = {}
    for d in dests:
        by.setdefault(wslot(topo, cores, d, a), []).append(d)
    return [(mask, wview(T, what, 0), T.sem["w%d" % s], [(d, wview(T, what, s)) for d in by[s]]) for s in sorted(by)]


def helper_program(g, core, T, topo, everyone):
    cores = list(T.cores)
    for a in everyone:
        hs = helpers(topo, cores, a, everyone) if a in cores else []
        if core not in hs:
            continue
        what = ("codes", "scales")[hs.index(core)]
        lo, hi, hand = engines(topo, cores, a)
        cnt = {"snd": 0}
        me, d = row(topo, cores, a).index(a), opposite(topo, cores, a)
        g.wait_ge(T.sem.xrl, len(bits(hi)) // 2)
        fused(g, core, T, topo, cnt, [(topo.mask(core, d), xview(T, what, me), T.sem["x%d" % me], [(d, xview(T, what, me))])])
        far = far_partners(topo, cores, a)
        if far:
            g.wait_ge(T.sem.rly, len(bits(hand)))
            for t in w_transfers(T, topo, cores, a, what, far, topo.mask(core, far[0])):
                fused(g, core, T, topo, cnt, [t])
        g.wait_ge(T.sem.snd, cnt["snd"])


def rank_program(g, core, T, topo):
    everyone = [c for c in range(256) if same_chip(topo, c, core)]
    if T.rank_of(core) is None:
        helper_program(g, core, T, topo, everyone)
        return
    cores = list(T.cores)
    R = row(topo, cores, core)
    me = R.index(core)
    near = [k for k in range(4) if k != me and same_chip(topo, core, R[k])]
    away = [k for k in range(4) if not same_chip(topo, core, R[k])]
    away.sort(key=lambda k: topo.die(R[k]) != topo.die(core))
    C = sorted(column(topo, cores, core), key=lambda c: wslot(topo, cores, core, c))
    lo, hi, hand = engines(topo, cores, core)
    nlo, nhi = len(bits(lo)), len(bits(hi))
    hi_a, hi_b = unbits(bits(hi)[::2]), unbits(bits(hi)[1::2])
    hs = helpers(topo, cores, core, everyone)
    straight = [d for d in C[1:] if topo.may_write(core, d)]
    cnt = {"v": 0, "s": 0, "snd": 0}

    def vi(ins):
        ins.then_inc(T.sem.v, 1)
        cnt["v"] += 1
        return cnt["v"]

    def si(ins):
        ins.then_inc(T.sem.s, 1)
        cnt["s"] += 1
        return cnt["s"]

    g.sync.dma_start(T.xt[:], T.x[:]).then_inc(T.sem.ld_x, 16)
    g.scalar.dma_start(T.tgs[:, 2 * me:2 * me + 2], T.tg[:]).then_inc(T.sem.ld_t, 16)
    g.scalar.dma_start(T.wt[:], T.w[:]).then_inc(T.sem.ld_w, 16)

    early, mid, late = [[(k, s, s + 1) for k in ks] for s, ks in enumerate((near + away, near + away, away + near))]
    first, last = (me, 0, 1), (me, 1, 3)
    foreign = early[:2] + mid[:2] + early[2:] + mid[2:] + late
    groups = [first] + foreign + [last]
    num = {gr: i for i, gr in enumerate(groups)}
    bank = {gr: i if i < 7 else 7 if gr == last else num[(gr[0], 0, 1)] for i, gr in enumerate(groups)}
    v, sc, pe = g.vector, g.scalar, g.tensor

    def cols(gr):
        k, s0, s1 = gr
        return k * NW + s0 * NC, k * NW + s1 * NC

    def psv(gr):
        return T.ps[:, 512 * bank[gr]:512 * bank[gr] + (gr[2] - gr[1]) * NC]

    def sums(gr):
        return T.land if gr[0] == me else T.st, 12 * gr[0] + 4 * gr[1]

    i_e0 = vi(v.memset(T.e0[:], -D))
    vi(v.memset(T.st[:], 0.0))
    vi(v.memset(T.mx[:], 1.0))
    vi(v.memset(T.mg[:, 0:1], MAGIC))
    vi(v.memset(T.mg[:, 1:2], -MAGIC))
    i_z = vi(v.memset(T.land[:, 12 * me:12 * me + 12], 0.0))
    v.wait_ge(T.sem.v, i_z)
    vi(v.memset(T.land[:, 12 * me + 9:12 * me + 10], BIG))
    v.wait_ge(T.sem.ld_x, 16)
    i_qx = vi(v.quantize_mx(T.xc[:, me * NT:(me + 1) * NT], T.xp[:, me * NT:(me + 1) * NT], T.xt[:]))
    v.wait_ge(T.sem.ld_w, 16)
    i_qw = vi(v.quantize_mx(T.wc[:, 0:NC], T.wp[:, 0:NC], T.wt[:]))

    def v_masks(ks):
        for k in ks:
            j = vi(v.tensor_scalar(T.key[:, k:k + 1], T.tgs[:, 2 * k:2 * k + 1], float(NC), T.tgs[:, 2 * k + 1:2 * k + 2],
                                   Op.mult, Op.add))
        v.wait_ge(T.sem.v, j)
        for k in ks:
            for s in range(3):
                o = k * NW + s * NC
                j = vi(v.tensor_scalar(T.mk[:, o:o + NC], T.cn[:], float(NC * T.rank_of(C[s])), T.key[:, k:k + 1],
                                       Op.add, Op.is_equal))
        return j

    def v_max(gr):
        i = num[gr]
        v.wait_ge(T.sem.pe, i + 1)
        return vi(v.tensor_reduce(T.mx[:, 2 * i:2 * i + 1], psv(gr), AxisListType.X, Op.max))

    def v_shift(gr, j):
        i = num[gr]
        buf, q = sums(gr)
        v.wait_ge(T.sem.v, j)
        return vi(v.tensor_tensor_scan(buf[:, q:q + 2], T.mx[:, 2 * i:2 * i + 2], T.mg[:], -A, Op.mult, Op.add))

    def v_pick(gr):
        a, b = cols(gr)
        return vi(v.tensor_tensor(T.pr[:, a:b], psv(gr), T.mk[:, a:b], Op.mult))

    def v_total(gr, j):
        a, b = cols(gr)
        buf, q = sums(gr)
        v.wait_ge(T.sem.v, j)
        return vi(v.tensor_reduce(buf[:, q + 3:q + 4], T.pr[:, a:b], AxisListType.X, Op.add))

    def s_exp(gr, j):
        a, b = cols(gr)
        buf, q = sums(gr)
        sc.wait_ge(T.sem.v, j)
        return si(sc.activation(T.ex[:, a:b], psv(gr), Fn.Exp, bias=buf[:, q + 1:q + 2], scale=A, accum_out=buf[:, q + 2:q + 3]))

    def s_total(gr, j):
        a, b = cols(gr)
        buf, q = sums(gr)
        sc.wait_ge(T.sem.v, j)
        return si(sc.activation(T.pr[:, a:b], T.pr[:, a:b], Fn.Copy, accum_out=buf[:, q + 3:q + 4]))

    sc.wait_ge(T.sem.v, i_e0)
    si(sc.activation(T.e1[:], T.e0[:], Fn.Exp))
    v.wait_ge(T.sem.cn_ok, 1)
    v.wait_ge(T.sem.ld_t, 16)
    j = v_masks([me])
    jm = v_max(first)
    v.wait_ge(T.sem.v, j)
    jp = v_pick(first)
    s_exp(first, v_shift(first, jm))
    v_total(first, jp)
    v.wait_ge(T.sem.tgin, 2 * nlo + nhi)
    j = v_masks(near + away)
    v.wait_ge(T.sem.v, j)
    freed, done_at = {}, {}
    for gr in foreign:
        k = gr[0]
        jm = v_max(gr)
        jp = v_pick(gr)
        j = s_exp(gr, v_shift(gr, jm))
        if gr in early:
            freed[k] = jp, j
        elif gr in mid:
            s_total((k, 0, 2), jp)
        else:
            done_at[k] = s_total(gr, jp)
    jm = v_max(last)
    jp = v_pick(last)
    i_own = s_exp(last, v_shift(last, jm))
    v_total(last, jp)
    si(sc.activation(T.e2[:], T.e1[:], Fn.Ln))

    seen = set()

    def pe_wait(name, n):
        if name not in seen:
            seen.add(name)
            pe.wait_ge(T.sem[name], n)
    pe_wait("v", i_qw)
    for gr in groups:
        k, s0, s1 = gr
        if k != me:
            pe_wait("x%d" % k, nhi if k in near else 2 * nlo)
        for s in range(max(s0, 1), s1):
            pe_wait("w%d" % s, 2 * nlo)
        if gr in late:
            pe.wait_ge(T.sem.v, freed[k][0])
            pe.wait_ge(T.sem.s, freed[k][1])
        pe.matmul_mx(psv(gr), T.xc[:, k * NT:(k + 1) * NT], T.xp[:, k * NT:(k + 1) * NT],
                     T.wc[:, s0 * NC:s1 * NC], T.wp[:, s0 * NC:s1 * NC], True, True).then_inc(T.sem.pe, 1)

    g.iota(T.cn[:], [[1, NC]], 0, 0, allow_small_or_imprecise_dtypes=True).then_inc(T.sem.cn_ok, 1)

    def send(tl):
        fused(g, core, T, topo, cnt, tl)
    g.wait_ge(T.sem.ld_t, 16)
    view = T.tgs[:, 2 * me:2 * me + 2]
    send([(lo, view, T.sem.tgin, [(R[k], view) for k in away]), (hi, view, T.sem.tgin, [(R[k], view) for k in near])])
    g.wait_ge(T.sem.v, i_qx)
    for h, what in zip(hs, ("codes", "scales")):
        view, sem = xview(T, what, me), T.sem["x%d" % me]
        send([(lo, view, sem, [(R[away[0]], view)]), (hi_a, view, sem, [(R[near[0]], view)]), (hi_b, view, T.sem.xrl, [(h, view)])])
    g.wait_ge(T.sem.v, i_qw)
    for h, what in zip(hs, ("codes", "scales")):
        tl = [(hand, wview(T, what, 0), T.sem.rly, [(h, wview(T, what, 0))])] if far_partners(topo, cores, core) else []
        send(tl + w_transfers(T, topo, cores, core, what, straight, lo))
    for k in away + near:
        g.wait_ge(T.sem.s, done_at[k])
        send([(hi if k in near else lo, T.st[:, 12 * k:12 * k + 12], T.sem["st%d" % me], [(R[k], T.land[:, 12 * me:12 * me + 12])])])
    g.wait_ge(T.sem.snd, cnt["snd"])

    v.wait_ge(T.sem.s, i_own)
    for k in near + away:
        v.wait_ge(T.sem["st%d" % k], nhi if k in near else nlo)
    v.wait_ge(T.sem.v, cnt["v"])
    B, S, TL = T.land[:, 1:48:4], T.land[:, 2:48:4], T.land[:, 3:48:4]
    j = vi(v.tensor_reduce(T.fb[:, 1:2], B, AxisListType.X, Op.min))
    vi(v.tensor_scalar(T.fe[:], S, T.e1[:], None, Op.mult))
    v.wait_ge(T.sem.v, j)
    jk = vi(v.tensor_scalar(T.fk[:], B, T.fb[:, 1:2], D / 2, Op.subtract, Op.is_lt))
    jq = vi(v.tensor_scalar(T.fq[:], B, T.fb[:, 1:2], D, Op.subtract, Op.is_equal))
    v.wait_ge(T.sem.v, jk)
    vi(v.tensor_tensor(T.fp[:, 0:12], T.fk[:], S, Op.mult))
    v.wait_ge(T.sem.v, jq)
    j = vi(v.tensor_tensor(T.fp[:, 12:24], T.fq[:], T.fe[:], Op.mult))
    v.wait_ge(T.sem.v, j)
    j = vi(v.tensor_reduce(T.fs[:], T.fp[:], AxisListType.X, Op.add))
    jt = vi(v.tensor_reduce(T.ft[:], TL, AxisListType.X, Op.add))
    sc.wait_ge(T.sem.v, j)
    j = si(sc.activation(T.fz[:], T.fs[:], Fn.Ln))
    v.wait_ge(T.sem.v, jt)
    jt = vi(v.tensor_scalar(T.fb[:, 0:1], T.ft[:], A, T.fb[:, 1:2], Op.mult, Op.add))
    v.wait_ge(T.sem.v, jt)
    v.wait_ge(T.sem.s, j)
    j = vi(v.tensor_scalar(T.yo[:], T.fb[:], T.fz[:], -1.0, Op.subtract, Op.mult))
    g.sync.wait_ge(T.sem.v, j)
    g.sync.dma_start(T.y[:], T.yo[:]).then_inc(T.sem.st_y, 16)
    g.sync.wait_ge(T.sem.st_y, 16)
